import numpy as np
import ml_dtypes


def mxq(x, axis, fmt="e4m3"):
    dtype, down = {"e4m3": (ml_dtypes.float8_e4m3fn, 7), "e5m2": (ml_dtypes.float8_e5m2, 14)}[fmt]
    v = np.moveaxis(np.asarray(x, np.float32).astype(ml_dtypes.bfloat16).astype(np.float64), axis, -1)
    blocks = v.reshape(v.shape[:-1] + (-1, 32))
    amax = np.abs(blocks).max(-1, keepdims=True)
    byte = np.maximum(np.where(amax > 0, np.frexp(amax)[1] - 1 + 127, 0) - down, 1)
    scale = np.exp2(byte - 127.0)
    codes = (blocks / scale).astype(np.float32).astype(dtype).astype(np.float64)
    return np.moveaxis((codes * scale).reshape(v.shape), -1, axis)


WIDE = False


def mx_kscale(k):
    if not WIDE:
        return np.ones(k)
    levels = np.array([10, -10, 5, -5, 0])
    if k % 512:
        return np.exp2(np.random.permutation(np.resize(levels, k // 32))).repeat(32)
    a = np.empty((k // 512, 16))
    for p in range(k // 512):
        a[p, :8] = np.random.permutation(np.resize(levels, 8))
        for g in range(8):
            far = levels[np.abs(levels - a[p, g]) >= 10]
            a[p, g + 8] = far[np.random.randint(len(far))]
    return np.exp2(a.ravel()).repeat(32)


def f64(x):
    return np.asarray(x).astype(np.float64)


def striped(idx):
    return np.tile(idx.reshape(-1, 16).T, (8, 1)).astype(np.uint16)


def unstriped(offs):
    return offs[:16].T.reshape(-1).astype(np.int64)


def striped8(idx):
    return np.concatenate([x.reshape(-1, 16).T for x in idx]).astype(np.uint16)


def runs(offs, k):
    lists = np.stack([offs[16 * r : 16 * r + 16].T.reshape(-1) for r in range(8)]).astype(np.int64)
    return lists[np.arange(k) % 512 // 64]


def pack_weight(w):
    k, n = w.shape
    w = f64(np.asarray(w, np.float32).astype(ml_dtypes.bfloat16)).reshape(k // 32, 32, n)
    amax = np.abs(w).max(1)
    byte = np.clip(np.where(amax > 0, np.frexp(amax)[1] - 1 + 127 - 7, 1), 1, 254)
    scaled = (w * np.exp2(127.0 - byte)[:, None, :]).reshape(k, n).astype(np.float32)
    words = np.ascontiguousarray(scaled.reshape(k // 512, 128, 4, n).transpose(0, 1, 3, 2)).astype(ml_dtypes.float8_e4m3fn).view(np.uint8)
    return words, np.ascontiguousarray(byte.astype(np.uint8).reshape(k // 512, 16, n))


def unpack_weight(words, scales):
    g, p, n, _ = words.shape
    vals = np.ascontiguousarray(words).view(ml_dtypes.float8_e4m3fn).astype(np.float64) * np.repeat(np.exp2(scales.astype(np.float64) - 127.0), 8, axis=1)[..., None]
    return vals.transpose(0, 1, 3, 2).reshape(g * 512, n)


def relu(v):
    return np.maximum(v, 0.0)

def planes(y):
    n, m = y.shape
    v = y.astype(np.float32).astype(ml_dtypes.bfloat16).astype(np.float64).reshape(n // 32, 32, m)
    top = np.abs(v).max(1)
    byte = np.clip(np.where(top > 0, np.frexp(top)[1] - 1 + 127 - 7, 1), 1, 254)
    codes = (v * np.exp2(127.0 - byte)[:, None, :]).reshape(n, m).astype(np.float32).astype(ml_dtypes.float8_e4m3fn).view(np.uint8)
    words = codes.reshape(n // 512, 128, 4, m).transpose(0, 1, 3, 2)
    return np.ascontiguousarray(words), np.ascontiguousarray(byte.astype(np.uint8).reshape(n // 512, 16, m))


K, T, S, N, H, J, W = 512, 2048, 512, 512, 512, 512, 256


def setup_inputs():
    n = np.random.standard_normal
    s = mx_kscale(K)[:, None]
    u = mx_kscale(H)
    packed_xT = pack_weight(n((K, T)) * s)
    packed_w1 = pack_weight(n((K, H)) / np.sqrt(K) / s)
    packed_w2 = pack_weight(n((H, N)) / np.sqrt(H) / u[:, None])
    packed_w3 = pack_weight(n((H, N)) / np.sqrt(H) / u[:, None])
    return {
        "x_words": packed_xT[0],
        "x_scales": packed_xT[1],
        "w1_words": packed_w1[0],
        "w1_scales": packed_w1[1],
        "tab": np.random.uniform(0.4, 1.4, (H, J)).astype(np.float32),
        "gn": (np.random.uniform(0.5, 1.5, (H, 1)) * u[:, None]).astype(np.float32),
        "w2_words": packed_w2[0],
        "w2_scales": packed_w2[1],
        "gm": (np.random.uniform(0.5, 1.5, (H, 1)) * u[:, None]).astype(np.float32),
        "w3_words": packed_w3[0],
        "w3_scales": packed_w3[1],
        "offs": striped(np.random.permutation(T)[:S]),
        "n1": striped8(np.random.randint(0, J, (8, S))),
        "n2": striped8(np.stack([np.random.permutation(S) for _ in range(8)])),
        "n3": striped8(np.stack([np.random.permutation(S) for _ in range(8)])),
        "n4": striped8(np.stack([np.random.permutation(S)[:W] for _ in range(8)])),
        "n5": striped8(np.stack([np.random.permutation(S)[:W] for _ in range(8)])),
    }


def reference(x_words, x_scales, w1_words, w1_scales, tab, gn, w2_words, w2_scales, gm, w3_words, w3_scales, offs, n1, n2, n3, n4, n5):
    xq = unpack_weight(x_words, x_scales)[:, unstriped(offs)]
    y = unpack_weight(w1_words, w1_scales).T @ xq
    rl = relu(y)
    ds = np.zeros((H, S))
    ds[np.arange(H)[:, None], runs(n3, H)] = rl
    z2 = f64(gm) * (ds - (0.5 * y))
    b = unpack_weight(w3_words, w3_scales).T @ mxq(z2, 0, "e4m3")
    z = f64(gn) * (y * (f64(tab)[np.arange(H)[:, None], runs(n1, H)]) - (0.5 * (y[np.arange(H)[:, None], runs(n2, H)])))
    a = unpack_weight(w2_words, w2_scales).T @ mxq(z, 0, "e4m3")
    ra = b[np.arange(N)[:, None], runs(n5, N)] - (0.5 * (a[np.arange(N)[:, None], runs(n4, N)]))
    out = a.copy()
    out[np.arange(N)[:, None], runs(n4, N)] = ra
    return (out,) + planes(out)

@@ -1,0 +1,230 @@
+from contextlib import ExitStack
+
+import concourse.mybir as mybir
+
+F32 = mybir.dt.float32
+BF16 = mybir.dt.bfloat16
+I32 = mybir.dt.int32
+U32 = mybir.dt.uint32
+U16 = mybir.dt.uint16
+U8 = mybir.dt.uint8
+FP8X4 = mybir.dt.float8_e4m3fn_x4
+ALU = mybir.AluOpType
+ACT = mybir.ActivationFunctionType
+
+P = 128
+PACK = 4
+T = 2048
+S = 512
+HALF = S // 2
+W = 256
+FLOPS = 3 * 2 * 512 * 512 * 512
+
+
+def tile_picked_forkputbkindgsend_none_po_kernel(
+    tc, x_words, x_scales, w1_words, w1_scales, tab, gn, w2_words, w2_scales, gm, w3_words, w3_scales,
+    offs, n1, n2, n3, n4, n5, out_0, out_1, out_2,
+):
+    nc = tc.nc
+    with ExitStack() as ctx:
+        lists = ctx.enter_context(tc.tile_pool(name="lists", bufs=1))
+        keep = ctx.enter_context(tc.tile_pool(name="keep", bufs=1))
+        psum = ctx.enter_context(tc.psum_pool(name="psum", bufs=1))
+
+        def load_list(src, name):
+            tile = lists.tile([P, src.shape[1]], U16, name=name)
+            nc.sync.dma_start(tile[:], src)
+            return tile
+
+        def load_words(src, name):
+            tile = keep.tile([P, src.shape[2]], I32, name=name, align_bytes=64)
+            nc.sync.dma_start(tile[:], src[0].rearrange("p n t -> p (n t)").bitcast(I32))
+            return tile
+
+        def cleared_plane(cols, name):
+            tile = keep.tile([P, cols], U8, name=name, align_bytes=64)
+            nc.vector.memset(tile[:].bitcast(I32), 0)
+            return tile
+
+        def load_scales(queue, tile, src, row):
+            for q in range(4):
+                queue.dma_start(
+                    tile[32 * q + row : 32 * q + row + 4, :].bitcast(I32),
+                    src[0, 4 * q : 4 * q + 4, :].bitcast(I32),
+                )
+
+        def deal(engine, order, raw, dtype, name):
+            tile = keep.tile([P, S], dtype, name=name, align_bytes=64)
+            engine.tensor_copy(
+                tile[:].rearrange("p (t m) -> " + order, t=PACK),
+                raw[:].rearrange("p (m t) -> " + order, t=PACK),
+            )
+            return tile
+
+        def load_gain(src, name):
+            tile = keep.tile([P, PACK], F32, name=name)
+            nc.sync.dma_start(tile[:], src.rearrange("(p t) o -> p (t o)", t=PACK))
+            return tile
+
+        def product(out, words, plane, row, t, codes, scales):
+            cols = slice(P * t, P * (t + 1))
+            nc.tensor.matmul_mx(
+                out, lhsT=words[:, cols].bitcast(FP8X4), lhsT_scale=plane[row:P, cols],
+                rhs=codes.bitcast(FP8X4), rhs_scale=scales, start=True, stop=True,
+            )
+
+        xs = cleared_plane(T, "xs")
+        w1s_raw = cleared_plane(S, "w1s_raw")
+        w23s_raw = cleared_plane(S, "w23s_raw")
+
+        tab_rows = tab.rearrange("(p t) j -> t p j", t=PACK)
+
+        def load_tab(t):
+            tile = keep.tile([P, S], F32, name="tab%d" % t)
+            nc.sync.dma_start(tile[:], tab_rows[t])
+            return tile
+
+        n1_t = load_list(n1, "n1_t")
+        tabs = [load_tab(0)]
+        load_scales(nc.sync, xs, x_scales, 0)
+        offs_t = load_list(offs, "offs_t")
+        xw = load_words(x_words, "xw")
+        w1w_raw = load_words(w1_words, "w1w_raw")
+        load_scales(nc.sync, w1s_raw, w1_scales, 0)
+        tabs += [load_tab(1), load_tab(2)]
+        n3_t = load_list(n3, "n3_t")
+        gn_t = load_gain(gn, "gn_t")
+        tabs += [load_tab(3)]
+        gm_t = load_gain(gm, "gm_t")
+        w3w_raw = load_words(w3_words, "w3w_raw")
+        w2w_raw = load_words(w2_words, "w2w_raw")
+        load_scales(nc.sync, w23s_raw, w3_scales, 0)
+        load_scales(nc.sync, w23s_raw, w2_scales, 4)
+        n2_t = load_list(n2, "n2_t")
+        n5_t = load_list(n5, "n5_t")
+        n4_t = load_list(n4, "n4_t")
+
+        gn_half = keep.tile([P, PACK], F32, name="gn_half")
+        nc.scalar.activation(gn_half[:], gn_t[:], ACT.Copy, scale=-0.5)
+
+        kinds = []
+
+        def pick_kinds(t):
+            tile = keep.tile([P, S], F32, name="kind%d" % t)
+            for h in range(2):
+                nc.vector.tensor_scalar(
+                    tile[:, HALF * h : HALF * (h + 1)], tabs[t][:].indirect(n1_t[:, 16 * h : 16 * (h + 1)]),
+                    -2.0, 0.0, ALU.mult, ALU.add,
+                )
+            kinds.append(tile)
+
+        xg = keep.tile([P, S], U32, name="xg", align_bytes=64)
+        xsg = keep.tile([P, S], U8, name="xsg", align_bytes=64)
+        pick_kinds(0)
+        nc.vector.tensor_copy(xsg[:], xs[:].indirect(offs_t[:]))
+        nc.vector.tensor_copy(xg[:], xw[:].bitcast(U32).indirect(offs_t[:]))
+        w1s = deal(nc.vector, "p m t", w1s_raw, U8, "w1s")
+        w1w = deal(nc.vector, "p m t", w1w_raw, I32, "w1w")
+        pick_kinds(1)
+        pick_kinds(2)
+
+        banks = [psum.tile([P, S], F32, name="y%d" % t, tag="ya%d" % t) for t in range(PACK)]
+        for t in range(PACK):
+            product(banks[t][:], w1w, w1s, 0, t, xg[:], xsg[:])
+
+        z2_bf = keep.tile([P, S, PACK], BF16, name="z2_bf", tag="z2_then_z", align_bytes=64)
+        gained, prods = [], []
+        for t in range(PACK):
+            rl = keep.tile([P, S], F32, name="rl%d" % t)
+            nc.scalar.activation(rl[:], banks[t][:], ACT.Relu)
+            neg_half = keep.tile([P, S], F32, name="neg_half%d" % t)
+            nc.scalar.activation(neg_half[:], banks[t][:], ACT.Copy, scale=-0.5)
+            yg = keep.tile([P, S], F32, name="yg%d" % t)
+            nc.scalar.activation(yg[:], banks[t][:], ACT.Copy, scale=gn_half[:, t : t + 1])
+            gained.append(yg)
+            ds = keep.tile([P, 2 * S], F32, name="ds%d" % t)
+            nc.vector.tensor_copy(ds[:].indirect(n3_t[:]), rl[:])
+            if t == 0:
+                pick_kinds(3)
+            prod = keep.tile([P, S], F32, name="prod%d" % t)
+            nc.gpsimd.tensor_tensor(prod[:], kinds[t][:], yg[:], ALU.mult)
+            prods.append(prod)
+            diff = keep.tile([P, S], F32, name="diff%d" % t)
+            adder = nc.vector if t == PACK - 1 else nc.gpsimd
+            adder.tensor_tensor(diff[:], ds[:, 0:S], neg_half[:], ALU.add)
+            nc.scalar.activation(z2_bf[:, :, t], diff[:], ACT.Copy, scale=gm_t[:, t : t + 1])
+            if t == 0:
+                w3w = deal(nc.gpsimd, "p t m", w3w_raw, I32, "w3w")
+                w2w = deal(nc.gpsimd, "p t m", w2w_raw, I32, "w2w")
+            if t == 1:
+                w23s = deal(nc.gpsimd, "p t m", w23s_raw, U8, "w23s")
+        z2_codes = keep.tile([P, S], U32, name="z2_codes", align_bytes=64)
+        z2_scales = keep.tile([P, S], U8, name="z2_scales", align_bytes=64)
+        nc.vector.quantize_mx(z2_codes[:].bitcast(FP8X4), z2_scales[:], z2_bf[:].rearrange("p j t -> p (j t)"))
+        bs = []
+        for t in range(PACK):
+            bank = psum.tile([P, S], F32, name="b%d" % t)
+            product(bank[:], w3w, w23s, 0, t, z2_codes[:], z2_scales[:])
+            b = keep.tile([P, S], F32, name="bsb%d" % t)
+            nc.scalar.copy(b[:], bank[:])
+            bs.append(b)
+
+        a_banks = [psum.tile([P, S], F32, name="a%d" % t, tag="ya%d" % t) for t in range(PACK)]
+        for h in range(2):
+            cols = slice(HALF * h, HALF * (h + 1))
+            entries = slice(16 * h, 16 * (h + 1))
+            z = keep.tile([P, PACK, HALF], F32, name="z%d" % h, tag=("z0", "z2_then_z")[h], align_bytes=64)
+            z_bf = keep.tile([P, HALF, PACK], BF16, name="z_bf%d" % h, tag="z_bf%d" % h, align_bytes=64)
+            for t in range(PACK):
+                nc.vector.tensor_tensor(z[:, t, :], gained[t][:].indirect(n2_t[:, entries]), prods[t][:, cols], ALU.add)
+            nc.scalar.copy(
+                z_bf[:].rearrange("p (c i) t -> p c t i", i=4),
+                z[:].rearrange("p t (c i) -> p c t i", i=4),
+            )
+            z_codes = keep.tile([P, HALF], U32, name="z_codes%d" % h, align_bytes=64)
+            z_scales = keep.tile([P, HALF], U8, name="z_scales%d" % h, align_bytes=64)
+            nc.vector.quantize_mx(z_codes[:].bitcast(FP8X4), z_scales[:], z_bf[:].rearrange("p j t -> p (j t)"))
+            for t in range(PACK):
+                product(a_banks[t][:, cols], w2w, w23s, 4, t, z_codes[:], z_scales[:])
+        outs = []
+        for t in range(PACK):
+            tile = keep.tile([P, S], F32, name="o%d" % t)
+            nc.scalar.copy(tile[:], a_banks[t][:])
+            outs.append(tile)
+
+        out_rows = out_0.rearrange("(p t) j -> t p j", t=PACK)
+        out_bf = keep.tile([P, S, PACK], BF16, name="out_bf", align_bytes=64)
+        picked_b = []
+        for t in range(PACK):
+            tag = ("picked_b0", "picked_b1", "z_bf0", "z_bf1")[t]
+            tile = keep.tile([P, W], F32, name="picked_b%d" % t, tag=tag, align_bytes=64)
+            nc.vector.tensor_copy(tile[:], bs[t][:].indirect(n5_t[:]))
+            picked_b.append(tile)
+        picked_a = []
+
+        def pick_a(t):
+            tile = keep.tile([P, W], F32, name="picked_a%d" % t)
+            nc.vector.tensor_scalar(tile[:], outs[t][:].indirect(n4_t[:]), -0.5, 0.0, ALU.mult, ALU.add)
+            picked_a.append(tile)
+
+        pick_a(0)
+        for t in range(PACK):
+            if t + 1 < PACK:
+                pick_a(t + 1)
+            nc.vector.tensor_tensor(outs[t][:].indirect(n4_t[:]), picked_b[t][:], picked_a[t][:], ALU.add)
+            nc.sync.dma_start(out_rows[t], outs[t][:])
+            for h in range(2):
+                cols = slice(HALF * h, HALF * (h + 1))
+                if t >= 2 and h == 0:
+                    nc.vector.tensor_copy(out_bf[:, cols, t], outs[t][:, cols])
+                else:
+                    nc.scalar.copy(out_bf[:, cols, t], outs[t][:, cols])
+        codes = keep.tile([P, S], U32, name="codes", align_bytes=64)
+        scales = keep.tile([P, S], U8, name="scales", align_bytes=64)
+        words_out = out_1[0].rearrange("p n t -> p (n t)").bitcast(I32)
+        for h in range(2):
+            cols = slice(HALF * h, HALF * (h + 1))
+            nc.vector.quantize_mx(codes[:, cols].bitcast(FP8X4), scales[:, cols], out_bf[:, cols, :].rearrange("p j t -> p (j t)"))
+            nc.scalar.dma_start(words_out[:, cols], codes[:, cols].bitcast(I32))
+        for q in range(4):
+            nc.sync.dma_start(out_2[0, 4 * q : 4 * q + 4, :].bitcast(I32), scales[32 * q : 32 * q + 4, :].bitcast(I32))

@@ -88,13 +88,13 @@ def tile_picked_forkputbkindgsend_none_po_kernel(
         tabs = [load_tab(0)]
         load_scales(nc.sync, xs, x_scales, 0)
         offs_t = load_list(offs, "offs_t")
+        tabs += [load_tab(1)]
         xw = load_words(x_words, "xw")
-        w1w_raw = load_words(w1_words, "w1w_raw")
         load_scales(nc.sync, w1s_raw, w1_scales, 0)
-        tabs += [load_tab(1), load_tab(2)]
+        w1w_raw = load_words(w1_words, "w1w_raw")
+        tabs += [load_tab(2), load_tab(3)]
         n3_t = load_list(n3, "n3_t")
         gn_t = load_gain(gn, "gn_t")
-        tabs += [load_tab(3)]
         gm_t = load_gain(gm, "gm_t")
         w3w_raw = load_words(w3_words, "w3w_raw")
         w2w_raw = load_words(w2_words, "w2w_raw")
@@ -110,7 +110,7 @@ def tile_picked_forkputbkindgsend_none_po_kernel(
         kinds = []
 
         def pick_kinds(t):
-            tile = keep.tile([P, S], F32, name="kind%d" % t)
+            tile = keep.tile([P, S], F32, name="kind%d" % t, tag="kind%d" % t, align_bytes=64)
             for h in range(2):
                 nc.vector.tensor_scalar(
                     tile[:, HALF * h : HALF * (h + 1)], tabs[t][:].indirect(n1_t[:, 16 * h : 16 * (h + 1)]),
@@ -122,42 +122,42 @@ def tile_picked_forkputbkindgsend_none_po_kernel(
         xsg = keep.tile([P, S], U8, name="xsg", align_bytes=64)
         pick_kinds(0)
         nc.vector.tensor_copy(xsg[:], xs[:].indirect(offs_t[:]))
-        nc.vector.tensor_copy(xg[:], xw[:].bitcast(U32).indirect(offs_t[:]))
-        w1s = deal(nc.vector, "p m t", w1s_raw, U8, "w1s")
-        w1w = deal(nc.vector, "p m t", w1w_raw, I32, "w1w")
         pick_kinds(1)
+        nc.vector.tensor_copy(xg[:], xw[:].bitcast(U32).indirect(offs_t[:]))
+        w1s = deal(nc.gpsimd, "p t m", w1s_raw, U8, "w1s")
+        w1w = deal(nc.gpsimd, "p t m", w1w_raw, I32, "w1w")
         pick_kinds(2)
+        pick_kinds(3)
 
         banks = [psum.tile([P, S], F32, name="y%d" % t, tag="ya%d" % t) for t in range(PACK)]
         for t in range(PACK):
             product(banks[t][:], w1w, w1s, 0, t, xg[:], xsg[:])
 
         z2_bf = keep.tile([P, S, PACK], BF16, name="z2_bf", tag="z2_then_z", align_bytes=64)
-        gained, prods = [], []
+        positive, gained, prods = [], [], []
         for t in range(PACK):
             rl = keep.tile([P, S], F32, name="rl%d" % t)
             nc.scalar.activation(rl[:], banks[t][:], ACT.Relu)
-            neg_half = keep.tile([P, S], F32, name="neg_half%d" % t)
-            nc.scalar.activation(neg_half[:], banks[t][:], ACT.Copy, scale=-0.5)
+            positive.append(rl)
             yg = keep.tile([P, S], F32, name="yg%d" % t)
             nc.scalar.activation(yg[:], banks[t][:], ACT.Copy, scale=gn_half[:, t : t + 1])
             gained.append(yg)
-            ds = keep.tile([P, 2 * S], F32, name="ds%d" % t)
-            nc.vector.tensor_copy(ds[:].indirect(n3_t[:]), rl[:])
-            if t == 0:
-                pick_kinds(3)
             prod = keep.tile([P, S], F32, name="prod%d" % t)
             nc.gpsimd.tensor_tensor(prod[:], kinds[t][:], yg[:], ALU.mult)
             prods.append(prod)
-            diff = keep.tile([P, S], F32, name="diff%d" % t)
+        for t in range(PACK):
+            neg_half = keep.tile([P, S], F32, name="neg_half%d" % t, tag="neg_half%d" % t, align_bytes=64)
+            nc.scalar.activation(neg_half[:], banks[t][:], ACT.Copy, scale=-0.5)
+            ds = keep.tile([P, 2 * S], F32, name="ds%d" % t)
+            nc.vector.tensor_copy(ds[:].indirect(n3_t[:]), positive[t][:])
+            tag = ("kind3", "kind2", "kind1", "neg_half2")[t]
+            diff = keep.tile([P, S], F32, name="diff%d" % t, tag=tag, align_bytes=64)
             adder = nc.vector if t == PACK - 1 else nc.gpsimd
             adder.tensor_tensor(diff[:], ds[:, 0:S], neg_half[:], ALU.add)
             nc.scalar.activation(z2_bf[:, :, t], diff[:], ACT.Copy, scale=gm_t[:, t : t + 1])
-            if t == 0:
-                w3w = deal(nc.gpsimd, "p t m", w3w_raw, I32, "w3w")
-                w2w = deal(nc.gpsimd, "p t m", w2w_raw, I32, "w2w")
-            if t == 1:
-                w23s = deal(nc.gpsimd, "p t m", w23s_raw, U8, "w23s")
+        w3w = deal(nc.gpsimd, "p t m", w3w_raw, I32, "w3w")
+        w23s = deal(nc.gpsimd, "p t m", w23s_raw, U8, "w23s")
+        w2w = deal(nc.gpsimd, "p t m", w2w_raw, I32, "w2w")
         z2_codes = keep.tile([P, S], U32, name="z2_codes", align_bytes=64)
         z2_scales = keep.tile([P, S], U8, name="z2_scales", align_bytes=64)
         nc.vector.quantize_mx(z2_codes[:].bitcast(FP8X4), z2_scales[:], z2_bf[:].rearrange("p j t -> p (j t)"))
@@ -173,7 +173,7 @@ def tile_picked_forkputbkindgsend_none_po_kernel(
         for h in range(2):
             cols = slice(HALF * h, HALF * (h + 1))
             entries = slice(16 * h, 16 * (h + 1))
-            z = keep.tile([P, PACK, HALF], F32, name="z%d" % h, tag=("z0", "z2_then_z")[h], align_bytes=64)
+            z = keep.tile([P, PACK, HALF], F32, name="z%d" % h, tag=("neg_half3", "z2_then_z")[h], align_bytes=64)
             z_bf = keep.tile([P, HALF, PACK], BF16, name="z_bf%d" % h, tag="z_bf%d" % h, align_bytes=64)
             for t in range(PACK):
                 nc.vector.tensor_tensor(z[:, t, :], gained[t][:].indirect(n2_t[:, entries]), prods[t][:, cols], ALU.add)

@@ -42,7 +42,7 @@ def tile_picked_forkputbkindgsend_none_po_kernel(
             return tile
 
         def cleared_plane(cols, name):
-            tile = keep.tile([P, cols], U8, name=name, align_bytes=64)
+            tile = keep.tile([P, cols], U8, name=name, tag=name, align_bytes=64)
             nc.vector.memset(tile[:].bitcast(I32), 0)
             return tile
 
@@ -80,8 +80,8 @@ def tile_picked_forkputbkindgsend_none_po_kernel(
         tab_rows = tab.rearrange("(p t) j -> t p j", t=PACK)
 
         def load_tab(t):
-            tile = keep.tile([P, S], F32, name="tab%d" % t)
-            nc.sync.dma_start(tile[:], tab_rows[t])
+            tile = keep.tile([P, 2 * S], F32, name="tab%d" % t)
+            nc.sync.dma_start(tile[:, 0:S], tab_rows[t])
             return tile
 
         n1_t = load_list(n1, "n1_t")
@@ -92,12 +92,13 @@ def tile_picked_forkputbkindgsend_none_po_kernel(
         xw = load_words(x_words, "xw")
         load_scales(nc.sync, w1s_raw, w1_scales, 0)
         w1w_raw = load_words(w1_words, "w1w_raw")
-        tabs += [load_tab(2), load_tab(3)]
-        n3_t = load_list(n3, "n3_t")
-        gn_t = load_gain(gn, "gn_t")
-        gm_t = load_gain(gm, "gm_t")
+        tabs += [load_tab(2)]
         w3w_raw = load_words(w3_words, "w3w_raw")
+        tabs += [load_tab(3)]
         w2w_raw = load_words(w2_words, "w2w_raw")
+        gn_t = load_gain(gn, "gn_t")
+        n3_t = load_list(n3, "n3_t")
+        gm_t = load_gain(gm, "gm_t")
         load_scales(nc.sync, w23s_raw, w3_scales, 0)
         load_scales(nc.sync, w23s_raw, w2_scales, 4)
         n2_t = load_list(n2, "n2_t")
@@ -111,11 +112,7 @@ def tile_picked_forkputbkindgsend_none_po_kernel(
 
         def pick_kinds(t):
             tile = keep.tile([P, S], F32, name="kind%d" % t, tag="kind%d" % t, align_bytes=64)
-            for h in range(2):
-                nc.vector.tensor_scalar(
-                    tile[:, HALF * h : HALF * (h + 1)], tabs[t][:].indirect(n1_t[:, 16 * h : 16 * (h + 1)]),
-                    -2.0, 0.0, ALU.mult, ALU.add,
-                )
+            nc.vector.tensor_scalar(tile[:], tabs[t][:].indirect(n1_t[:]), -2.0, 0.0, ALU.mult, ALU.add)
             kinds.append(tile)
 
         xg = keep.tile([P, S], U32, name="xg", align_bytes=64)
@@ -124,8 +121,8 @@ def tile_picked_forkputbkindgsend_none_po_kernel(
         nc.vector.tensor_copy(xsg[:], xs[:].indirect(offs_t[:]))
         pick_kinds(1)
         nc.vector.tensor_copy(xg[:], xw[:].bitcast(U32).indirect(offs_t[:]))
-        w1s = deal(nc.gpsimd, "p t m", w1s_raw, U8, "w1s")
-        w1w = deal(nc.gpsimd, "p t m", w1w_raw, I32, "w1w")
+        w1s = deal(nc.vector, "p m t", w1s_raw, U8, "w1s")
+        w1w = deal(nc.vector, "p m t", w1w_raw, I32, "w1w")
         pick_kinds(2)
         pick_kinds(3)
 
@@ -134,6 +131,8 @@ def tile_picked_forkputbkindgsend_none_po_kernel(
             product(banks[t][:], w1w, w1s, 0, t, xg[:], xsg[:])
 
         z2_bf = keep.tile([P, S, PACK], BF16, name="z2_bf", tag="z2_then_z", align_bytes=64)
+        w3w = deal(nc.gpsimd, "p t m", w3w_raw, I32, "w3w")
+        w2w = deal(nc.gpsimd, "p t m", w2w_raw, I32, "w2w")
         positive, gained, prods = [], [], []
         for t in range(PACK):
             rl = keep.tile([P, S], F32, name="rl%d" % t)
@@ -150,26 +149,34 @@ def tile_picked_forkputbkindgsend_none_po_kernel(
             nc.scalar.activation(neg_half[:], banks[t][:], ACT.Copy, scale=-0.5)
             ds = keep.tile([P, 2 * S], F32, name="ds%d" % t)
             nc.vector.tensor_copy(ds[:].indirect(n3_t[:]), positive[t][:])
-            tag = ("kind3", "kind2", "kind1", "neg_half2")[t]
+            tag = ("kind3", "kind2", "w23s_raw", "neg_half2")[t]
             diff = keep.tile([P, S], F32, name="diff%d" % t, tag=tag, align_bytes=64)
             adder = nc.vector if t == PACK - 1 else nc.gpsimd
             adder.tensor_tensor(diff[:], ds[:, 0:S], neg_half[:], ALU.add)
             nc.scalar.activation(z2_bf[:, :, t], diff[:], ACT.Copy, scale=gm_t[:, t : t + 1])
-        w3w = deal(nc.gpsimd, "p t m", w3w_raw, I32, "w3w")
-        w23s = deal(nc.gpsimd, "p t m", w23s_raw, U8, "w23s")
-        w2w = deal(nc.gpsimd, "p t m", w2w_raw, I32, "w2w")
+            if t == 1:
+                w23s = deal(nc.gpsimd, "p t m", w23s_raw, U8, "w23s")
         z2_codes = keep.tile([P, S], U32, name="z2_codes", align_bytes=64)
         z2_scales = keep.tile([P, S], U8, name="z2_scales", align_bytes=64)
         nc.vector.quantize_mx(z2_codes[:].bitcast(FP8X4), z2_scales[:], z2_bf[:].rearrange("p j t -> p (j t)"))
-        bs = []
+        bs, b_banks = [], []
         for t in range(PACK):
             bank = psum.tile([P, S], F32, name="b%d" % t)
             product(bank[:], w3w, w23s, 0, t, z2_codes[:], z2_scales[:])
-            b = keep.tile([P, S], F32, name="bsb%d" % t)
-            nc.scalar.copy(b[:], bank[:])
+            b_banks.append(bank)
+
+        def keep_b(t, tag):
+            b = keep.tile([P, S], F32, name="bsb%d" % t, tag=tag, align_bytes=64)
+            nc.scalar.copy(b[:], b_banks[t][:])
             bs.append(b)
 
-        a_banks = [psum.tile([P, S], F32, name="a%d" % t, tag="ya%d" % t) for t in range(PACK)]
+        for t in range(PACK - 1):
+            keep_b(t, "bsb%d" % t)
+
+        a_banks = [
+            [psum.tile([P, 2, HALF], F32, name="a%d%d" % (h, u), tag="ya%d" % (2 * h + u)) for u in range(2)]
+            for h in range(2)
+        ]
         for h in range(2):
             cols = slice(HALF * h, HALF * (h + 1))
             entries = slice(16 * h, 16 * (h + 1))
@@ -185,21 +192,24 @@ def tile_picked_forkputbkindgsend_none_po_kernel(
             z_scales = keep.tile([P, HALF], U8, name="z_scales%d" % h, align_bytes=64)
             nc.vector.quantize_mx(z_codes[:].bitcast(FP8X4), z_scales[:], z_bf[:].rearrange("p j t -> p (j t)"))
             for t in range(PACK):
-                product(a_banks[t][:, cols], w2w, w23s, 4, t, z_codes[:], z_scales[:])
+                product(a_banks[h][t // 2][:, t % 2, :], w2w, w23s, 4, t, z_codes[:], z_scales[:])
+        keep_b(PACK - 1, "z2_then_z")
         outs = []
         for t in range(PACK):
             tile = keep.tile([P, S], F32, name="o%d" % t)
-            nc.scalar.copy(tile[:], a_banks[t][:])
+            for h in range(2):
+                cols = slice(HALF * h, HALF * (h + 1))
+                nc.scalar.copy(tile[:, cols], a_banks[h][t // 2][:, t % 2, :])
             outs.append(tile)
 
         out_rows = out_0.rearrange("(p t) j -> t p j", t=PACK)
         out_bf = keep.tile([P, S, PACK], BF16, name="out_bf", align_bytes=64)
         picked_b = []
-        for t in range(PACK):
-            tag = ("picked_b0", "picked_b1", "z_bf0", "z_bf1")[t]
-            tile = keep.tile([P, W], F32, name="picked_b%d" % t, tag=tag, align_bytes=64)
-            nc.vector.tensor_copy(tile[:], bs[t][:].indirect(n5_t[:]))
-            picked_b.append(tile)
+        for pair in range(2):
+            tile = keep.tile([P, 2, W], F32, name="picked_b%d" % pair, tag="z_bf%d" % pair, align_bytes=64)
+            for u in range(2):
+                nc.vector.tensor_copy(tile[:, u, :], bs[2 * pair + u][:].indirect(n5_t[:]))
+                picked_b.append(tile[:, u, :])
         picked_a = []
 
         def pick_a(t):
@@ -211,7 +221,7 @@ def tile_picked_forkputbkindgsend_none_po_kernel(
         for t in range(PACK):
             if t + 1 < PACK:
                 pick_a(t + 1)
-            nc.vector.tensor_tensor(outs[t][:].indirect(n4_t[:]), picked_b[t][:], picked_a[t][:], ALU.add)
+            nc.vector.tensor_tensor(outs[t][:].indirect(n4_t[:]), picked_b[t], picked_a[t][:], ALU.add)
             nc.sync.dma_start(out_rows[t], outs[t][:])
             for h in range(2):
                 cols = slice(HALF * h, HALF * (h + 1))

from contextlib import ExitStack

import concourse.mybir as mybir

F32 = mybir.dt.float32
BF16 = mybir.dt.bfloat16
I32 = mybir.dt.int32
U32 = mybir.dt.uint32
U16 = mybir.dt.uint16
U8 = mybir.dt.uint8
FP8X4 = mybir.dt.float8_e4m3fn_x4
ALU = mybir.AluOpType
ACT = mybir.ActivationFunctionType

P = 128
PACK = 4
T = 2048
S = 512
HALF = S // 2
W = 256
FLOPS = 3 * 2 * 512 * 512 * 512


def tile_picked_forkputbkindgsend_none_po_kernel(
    tc, x_words, x_scales, w1_words, w1_scales, tab, gn, w2_words, w2_scales, gm, w3_words, w3_scales,
    offs, n1, n2, n3, n4, n5, out_0, out_1, out_2,
):
    nc = tc.nc
    with ExitStack() as ctx:
        lists = ctx.enter_context(tc.tile_pool(name="lists", bufs=1))
        keep = ctx.enter_context(tc.tile_pool(name="keep", bufs=1))
        psum = ctx.enter_context(tc.psum_pool(name="psum", bufs=1))

        def load_list(src, name):
            tile = lists.tile([P, src.shape[1]], U16, name=name)
            nc.sync.dma_start(tile[:], src)
            return tile

        def load_words(src, name):
            tile = keep.tile([P, src.shape[2]], I32, name=name, align_bytes=64)
            nc.sync.dma_start(tile[:], src[0].rearrange("p n t -> p (n t)").bitcast(I32))
            return tile

        def cleared_plane(cols, name):
            tile = keep.tile([P, cols], U8, name=name, tag=name, align_bytes=64)
            nc.vector.memset(tile[:].bitcast(I32), 0)
            return tile

        def load_scales(queue, tile, src, row):
            for q in range(4):
                queue.dma_start(
                    tile[32 * q + row : 32 * q + row + 4, :].bitcast(I32),
                    src[0, 4 * q : 4 * q + 4, :].bitcast(I32),
                )

        def deal(engine, order, raw, dtype, name):
            tile = keep.tile([P, S], dtype, name=name, align_bytes=64)
            engine.tensor_copy(
                tile[:].rearrange("p (t m) -> " + order, t=PACK),
                raw[:].rearrange("p (m t) -> " + order, t=PACK),
            )
            return tile

        def load_gain(src, name):
            tile = keep.tile([P, PACK], F32, name=name)
            nc.sync.dma_start(tile[:], src.rearrange("(p t) o -> p (t o)", t=PACK))
            return tile

        def product(out, words, plane, row, t, codes, scales):
            cols = slice(P * t, P * (t + 1))
            nc.tensor.matmul_mx(
                out, lhsT=words[:, cols].bitcast(FP8X4), lhsT_scale=plane[row:P, cols],
                rhs=codes.bitcast(FP8X4), rhs_scale=scales, start=True, stop=True,
            )

        xs = cleared_plane(T, "xs")
        w1s_raw = cleared_plane(S, "w1s_raw")
        w23s_raw = cleared_plane(S, "w23s_raw")

        tab_rows = tab.rearrange("(p t) j -> t p j", t=PACK)

        def load_tab(t):
            tile = keep.tile([P, 2 * S], F32, name="tab%d" % t)
            nc.sync.dma_start(tile[:, 0:S], tab_rows[t])
            return tile

        n1_t = load_list(n1, "n1_t")
        tabs = [load_tab(0)]
        load_scales(nc.sync, xs, x_scales, 0)
        offs_t = load_list(offs, "offs_t")
        tabs += [load_tab(1)]
        xw = load_words(x_words, "xw")
        load_scales(nc.sync, w1s_raw, w1_scales, 0)
        w1w_raw = load_words(w1_words, "w1w_raw")
        tabs += [load_tab(2)]
        w3w_raw = load_words(w3_words, "w3w_raw")
        tabs += [load_tab(3)]
        w2w_raw = load_words(w2_words, "w2w_raw")
        gn_t = load_gain(gn, "gn_t")
        n3_t = load_list(n3, "n3_t")
        gm_t = load_gain(gm, "gm_t")
        load_scales(nc.sync, w23s_raw, w3_scales, 0)
        load_scales(nc.sync, w23s_raw, w2_scales, 4)
        n2_t = load_list(n2, "n2_t")
        n5_t = load_list(n5, "n5_t")
        n4_t = load_list(n4, "n4_t")

        gn_half = keep.tile([P, PACK], F32, name="gn_half")
        nc.scalar.activation(gn_half[:], gn_t[:], ACT.Copy, scale=-0.5)

        kinds = []

        def pick_kinds(t):
            tile = keep.tile([P, S], F32, name="kind%d" % t, tag="kind%d" % t, align_bytes=64)
            nc.vector.tensor_scalar(tile[:], tabs[t][:].indirect(n1_t[:]), -2.0, 0.0, ALU.mult, ALU.add)
            kinds.append(tile)

        xg = keep.tile([P, S], U32, name="xg", align_bytes=64)
        xsg = keep.tile([P, S], U8, name="xsg", align_bytes=64)
        pick_kinds(0)
        nc.vector.tensor_copy(xsg[:], xs[:].indirect(offs_t[:]))
        pick_kinds(1)
        nc.vector.tensor_copy(xg[:], xw[:].bitcast(U32).indirect(offs_t[:]))
        w1s = deal(nc.vector, "p m t", w1s_raw, U8, "w1s")
        w1w = deal(nc.vector, "p m t", w1w_raw, I32, "w1w")
        pick_kinds(2)
        pick_kinds(3)

        banks = [psum.tile([P, S], F32, name="y%d" % t, tag="ya%d" % t) for t in range(PACK)]
        for t in range(PACK):
            product(banks[t][:], w1w, w1s, 0, t, xg[:], xsg[:])

        z2_bf = keep.tile([P, S, PACK], BF16, name="z2_bf", tag="z2_then_z", align_bytes=64)
        w3w = deal(nc.gpsimd, "p t m", w3w_raw, I32, "w3w")
        w2w = deal(nc.gpsimd, "p t m", w2w_raw, I32, "w2w")
        positive, gained, prods = [], [], []
        for t in range(PACK):
            rl = keep.tile([P, S], F32, name="rl%d" % t)
            nc.scalar.activation(rl[:], banks[t][:], ACT.Relu)
            positive.append(rl)
            yg = keep.tile([P, S], F32, name="yg%d" % t)
            nc.scalar.activation(yg[:], banks[t][:], ACT.Copy, scale=gn_half[:, t : t + 1])
            gained.append(yg)
            prod = keep.tile([P, S], F32, name="prod%d" % t)
            nc.gpsimd.tensor_tensor(prod[:], kinds[t][:], yg[:], ALU.mult)
            prods.append(prod)
        for t in range(PACK):
            neg_half = keep.tile([P, S], F32, name="neg_half%d" % t, tag="neg_half%d" % t, align_bytes=64)
            nc.scalar.activation(neg_half[:], banks[t][:], ACT.Copy, scale=-0.5)
            ds = keep.tile([P, 2 * S], F32, name="ds%d" % t)
            nc.vector.tensor_copy(ds[:].indirect(n3_t[:]), positive[t][:])
            tag = ("kind3", "kind2", "w23s_raw", "neg_half2")[t]
            diff = keep.tile([P, S], F32, name="diff%d" % t, tag=tag, align_bytes=64)
            adder = nc.vector if t == PACK - 1 else nc.gpsimd
            adder.tensor_tensor(diff[:], ds[:, 0:S], neg_half[:], ALU.add)
            nc.scalar.activation(z2_bf[:, :, t], diff[:], ACT.Copy, scale=gm_t[:, t : t + 1])
            if t == 1:
                w23s = deal(nc.gpsimd, "p t m", w23s_raw, U8, "w23s")
        z2_codes = keep.tile([P, S], U32, name="z2_codes", align_bytes=64)
        z2_scales = keep.tile([P, S], U8, name="z2_scales", align_bytes=64)
        nc.vector.quantize_mx(z2_codes[:].bitcast(FP8X4), z2_scales[:], z2_bf[:].rearrange("p j t -> p (j t)"))
        bs, b_banks = [], []
        for t in range(PACK):
            bank = psum.tile([P, S], F32, name="b%d" % t)
            product(bank[:], w3w, w23s, 0, t, z2_codes[:], z2_scales[:])
            b_banks.append(bank)

        def keep_b(t, tag):
            b = keep.tile([P, S], F32, name="bsb%d" % t, tag=tag, align_bytes=64)
            nc.scalar.copy(b[:], b_banks[t][:])
            bs.append(b)

        for t in range(PACK - 1):
            keep_b(t, "bsb%d" % t)

        a_banks = [
            [psum.tile([P, 2, HALF], F32, name="a%d%d" % (h, u), tag="ya%d" % (2 * h + u)) for u in range(2)]
            for h in range(2)
        ]
        for h in range(2):
            cols = slice(HALF * h, HALF * (h + 1))
            entries = slice(16 * h, 16 * (h + 1))
            z = keep.tile([P, PACK, HALF], F32, name="z%d" % h, tag=("neg_half3", "z2_then_z")[h], align_bytes=64)
            z_bf = keep.tile([P, HALF, PACK], BF16, name="z_bf%d" % h, tag="z_bf%d" % h, align_bytes=64)
            for t in range(PACK):
                nc.vector.tensor_tensor(z[:, t, :], gained[t][:].indirect(n2_t[:, entries]), prods[t][:, cols], ALU.add)
            nc.scalar.copy(
                z_bf[:].rearrange("p (c i) t -> p c t i", i=4),
                z[:].rearrange("p t (c i) -> p c t i", i=4),
            )
            z_codes = keep.tile([P, HALF], U32, name="z_codes%d" % h, align_bytes=64)
            z_scales = keep.tile([P, HALF], U8, name="z_scales%d" % h, align_bytes=64)
            nc.vector.quantize_mx(z_codes[:].bitcast(FP8X4), z_scales[:], z_bf[:].rearrange("p j t -> p (j t)"))
            for t in range(PACK):
                product(a_banks[h][t // 2][:, t % 2, :], w2w, w23s, 4, t, z_codes[:], z_scales[:])
        keep_b(PACK - 1, "z2_then_z")
        outs = []
        for t in range(PACK):
            tile = keep.tile([P, S], F32, name="o%d" % t)
            for h in range(2):
                cols = slice(HALF * h, HALF * (h + 1))
                nc.scalar.copy(tile[:, cols], a_banks[h][t // 2][:, t % 2, :])
            outs.append(tile)

        out_rows = out_0.rearrange("(p t) j -> t p j", t=PACK)
        out_bf = keep.tile([P, S, PACK], BF16, name="out_bf", align_bytes=64)
        picked_b = []
        for pair in range(2):
            tile = keep.tile([P, 2, W], F32, name="picked_b%d" % pair, tag="z_bf%d" % pair, align_bytes=64)
            for u in range(2):
                nc.vector.tensor_copy(tile[:, u, :], bs[2 * pair + u][:].indirect(n5_t[:]))
                picked_b.append(tile[:, u, :])
        picked_a = []

        def pick_a(t):
            tile = keep.tile([P, W], F32, name="picked_a%d" % t)
            nc.vector.tensor_scalar(tile[:], outs[t][:].indirect(n4_t[:]), -0.5, 0.0, ALU.mult, ALU.add)
            picked_a.append(tile)

        pick_a(0)
        for t in range(PACK):
            if t + 1 < PACK:
                pick_a(t + 1)
            nc.vector.tensor_tensor(outs[t][:].indirect(n4_t[:]), picked_b[t], picked_a[t][:], ALU.add)
            nc.sync.dma_start(out_rows[t], outs[t][:])
            for h in range(2):
                cols = slice(HALF * h, HALF * (h + 1))
                if t >= 2 and h == 0:
                    nc.vector.tensor_copy(out_bf[:, cols, t], outs[t][:, cols])
                else:
                    nc.scalar.copy(out_bf[:, cols, t], outs[t][:, cols])
        codes = keep.tile([P, S], U32, name="codes", align_bytes=64)
        scales = keep.tile([P, S], U8, name="scales", align_bytes=64)
        words_out = out_1[0].rearrange("p n t -> p (n t)").bitcast(I32)
        for h in range(2):
            cols = slice(HALF * h, HALF * (h + 1))
            nc.vector.quantize_mx(codes[:, cols].bitcast(FP8X4), scales[:, cols], out_bf[:, cols, :].rearrange("p j t -> p (j t)"))
            nc.scalar.dma_start(words_out[:, cols], codes[:, cols].bitcast(I32))
        for q in range(4):
            nc.sync.dma_start(out_2[0, 4 * q : 4 * q + 4, :].bitcast(I32), scales[32 * q : 32 * q + 4, :].bitcast(I32))
